import numpy as np
import ml_dtypes


def mxq(x, axis, fmt="e4m3"):
    dtype, down = {"e4m3": (ml_dtypes.float8_e4m3fn, 7), "e5m2": (ml_dtypes.float8_e5m2, 14)}[fmt]
    v = np.moveaxis(np.asarray(x, np.float32).astype(ml_dtypes.bfloat16).astype(np.float64), axis, -1)
    blocks = v.reshape(v.shape[:-1] + (-1, 32))
    amax = np.abs(blocks).max(-1, keepdims=True)
    byte = np.maximum(np.where(amax > 0, np.frexp(amax)[1] - 1 + 127, 0) - down, 1)
    scale = np.exp2(byte - 127.0)
    codes = (blocks / scale).astype(np.float32).astype(dtype).astype(np.float64)
    return np.moveaxis((codes * scale).reshape(v.shape), -1, axis)


WIDE = False


def mx_kscale(k):
    if not WIDE:
        return np.ones(k)
    levels = np.array([10, -10, 5, -5, 0])
    if k % 512:
        return np.exp2(np.random.permutation(np.resize(levels, k // 32))).repeat(32)
    a = np.empty((k // 512, 16))
    for p in range(k // 512):
        a[p, :8] = np.random.permutation(np.resize(levels, 8))
        for g in range(8):
            far = levels[np.abs(levels - a[p, g]) >= 10]
            a[p, g + 8] = far[np.random.randint(len(far))]
    return np.exp2(a.ravel()).repeat(32)


def f64(x):
    return np.asarray(x).astype(np.float64)


def striped(idx):
    return np.tile(idx.reshape(-1, 16).T, (8, 1)).astype(np.uint16)


def unstriped(offs):
    return offs[:16].T.reshape(-1).astype(np.int64)


def striped8(idx):
    return np.concatenate([x.reshape(-1, 16).T for x in idx]).astype(np.uint16)


def runs(offs, k):
    lists = np.stack([offs[16 * r : 16 * r + 16].T.reshape(-1) for r in range(8)]).astype(np.int64)
    return lists[np.arange(k) % 512 // 64]


def pack_weight(w):
    k, n = w.shape
    w = f64(np.asarray(w, np.float32).astype(ml_dtypes.bfloat16)).reshape(k // 32, 32, n)
    amax = np.abs(w).max(1)
    byte = np.clip(np.where(amax > 0, np.frexp(amax)[1] - 1 + 127 - 7, 1), 1, 254)
    scaled = (w * np.exp2(127.0 - byte)[:, None, :]).reshape(k, n).astype(np.float32)
    words = np.ascontiguousarray(scaled.reshape(k // 512, 128, 4, n).transpose(0, 1, 3, 2)).astype(ml_dtypes.float8_e4m3fn).view(np.uint8)
    return words, np.ascontiguousarray(byte.astype(np.uint8).reshape(k // 512, 16, n))


def unpack_weight(words, scales):
    g, p, n, _ = words.shape
    vals = np.ascontiguousarray(words).view(ml_dtypes.float8_e4m3fn).astype(np.float64) * np.repeat(np.exp2(scales.astype(np.float64) - 127.0), 8, axis=1)[..., None]
    return vals.transpose(0, 1, 3, 2).reshape(g * 512, n)


def sigmoid(v):
    return 1.0 / (1.0 + np.exp(-np.maximum(v, -700.0)))

def planes(y):
    n, m = y.shape
    v = y.astype(np.float32).astype(ml_dtypes.bfloat16).astype(np.float64).reshape(n // 32, 32, m)
    top = np.abs(v).max(1)
    byte = np.clip(np.where(top > 0, np.frexp(top)[1] - 1 + 127 - 7, 1), 1, 254)
    codes = (v * np.exp2(127.0 - byte)[:, None, :]).reshape(n, m).astype(np.float32).astype(ml_dtypes.float8_e4m3fn).view(np.uint8)
    words = codes.reshape(n // 512, 128, 4, m).transpose(0, 1, 3, 2)
    return np.ascontiguousarray(words), np.ascontiguousarray(byte.astype(np.uint8).reshape(n // 512, 16, m))


K, T, S, H = 512, 2048, 512, 512


def setup_inputs():
    n = np.random.standard_normal
    s = mx_kscale(K)[:, None]
    u = mx_kscale(S)
    packed_xT = pack_weight(n((K, T)) * s)
    return {
        "x_words": packed_xT[0],
        "x_scales": packed_xT[1],
        "wa": (n((K, H)) / np.sqrt(K) / s).astype(np.float32),
        "wb": (n((K, H)) / np.sqrt(K) / s).astype(np.float32),
        "sl": np.random.uniform(1.0, 2.0, (S, 1)).astype(np.float32),
        "th": (0.5 * n((S, 1))).astype(np.float32),
        "gt": (np.random.uniform(0.5, 1.5, (S, 1)) * u[:, None]).astype(np.float32),
        "gi": (np.random.uniform(0.5, 1.5, (S, 1)) / u[:, None]).astype(np.float32),
        "tau": np.random.uniform(0.3, 0.9, (H, 1)).astype(np.float32),
        "offs": striped(np.random.permutation(T)[:S]),
        "two": striped(np.random.permutation(T)[:S]),
        "n1": striped8(np.stack([np.random.permutation(H) for _ in range(8)])),
        "n2": striped8(np.stack([np.random.permutation(H) for _ in range(8)])),
        "n3": striped8(np.stack([np.random.permutation(H) for _ in range(8)])),
        "n4": striped8(np.stack([np.random.permutation(H) for _ in range(8)])),
    }


def reference(x_words, x_scales, wa, wb, sl, th, gt, gi, tau, offs, two, n1, n2, n3, n4):
    xq = unpack_weight(x_words, x_scales)[:, unstriped(offs)]
    a = xq.T @ mxq(f64(wa), 0, "e4m3")
    x_two = unpack_weight(x_words, x_scales)[:, unstriped(two)]
    b = x_two.T @ mxq(f64(wb), 0, "e4m3")
    sg = sigmoid(f64(sl) * (b[np.arange(S)[:, None], runs(n1, S)] - f64(th)))
    z = f64(gt) * (a * sg - (0.5 * (a[np.arange(S)[:, None], runs(n2, S)])))
    z2 = f64(gi) * b
    cv = 0.0625 * ((mxq(z, 0, "e4m3").T @ mxq(z2, 0, "e4m3")))
    top = cv.max(axis=1, keepdims=True)
    ea = np.exp(f64(tau) * (cv[np.arange(H)[:, None], runs(n3, H)] - top))
    sm = cv * ea
    ds = np.zeros((H, H))
    ds[np.arange(H)[:, None], runs(n4, H)] = sm
    out_0 = 2.0 * ds - (0.5 * cv)
    return (out_0,) + planes(out_0)

@@ -1,0 +1,268 @@
+from contextlib import ExitStack
+
+import concourse.mybir as mybir
+
+K, T, S, H = 512, 2048, 512, 512
+FLOPS = 3 * 2 * 512 * 512 * 512
+
+F32 = mybir.dt.float32
+BF16 = mybir.dt.bfloat16
+I32 = mybir.dt.int32
+U32 = mybir.dt.uint32
+U16 = mybir.dt.uint16
+U8 = mybir.dt.uint8
+FP8X4 = mybir.dt.float8_e4m3fn_x4
+ALU = mybir.AluOpType
+ACT = mybir.ActivationFunctionType
+
+P = 128
+PACK = 4
+HALF = H // 2
+LIST_COLS = S // 16
+
+
+def list_slice(offsets, a, b):
+    return offsets[:, a // 16 : b // 16]
+
+
+def tile_picked_momtgxbesd_none_po_kernel(
+    tc, x_words, x_scales, wa, wb, sl, th, gt, gi, tau, offs, two, n1, n2, n3, n4, out_0, out_1, out_2
+):
+    nc = tc.nc
+    with ExitStack() as ctx:
+        lists = ctx.enter_context(tc.tile_pool(name="lists", bufs=1))
+        sb = ctx.enter_context(tc.tile_pool(name="sb", bufs=1))
+        psum = ctx.enter_context(tc.psum_pool(name="psum", bufs=1))
+
+        def load_list(name, src):
+            tile = lists.tile([P, LIST_COLS], U16, name=name)
+            nc.sync.dma_start(tile[:], src)
+            return tile
+
+        def load_rows(name, src):
+            tile = sb.tile([P, PACK], F32, name=name)
+            nc.gpsimd.dma_start(tile[:], src.rearrange("(p t) o -> p (t o)", t=PACK))
+            return tile
+
+        def load_weight(name, src):
+            tile = sb.tile([P, PACK, H], F32, name=name)
+            nc.sync.dma_start(tile[:], src.rearrange("(p j) c -> p j c", j=PACK))
+            return tile
+
+        def interleave(name, copy, planes):
+            grouped = sb.tile([P, planes.shape[2], PACK], BF16, name=name, align_bytes=64)
+            copy(
+                grouped[:].rearrange("p (c i) t -> p c t i", i=4),
+                planes.rearrange("p t (c i) -> p c t i", i=4),
+            )
+            return grouped[:].rearrange("p c t -> p (c t)")
+
+        def mx_tiles(name):
+            codes = sb.tile([P, H], U32, name=f"{name}_codes", align_bytes=64)
+            scales = sb.tile([P, H], U8, name=f"{name}_scales", align_bytes=64)
+            return codes, scales
+
+        def quantize(operand, a, b, grouped):
+            nc.vector.quantize_mx(out=operand[0][:, a:b].bitcast(FP8X4), scales=operand[1][:, a:b], in_=grouped)
+
+        def gather_dealt(picked, table, offsets, a, b):
+            dealt = picked[:].rearrange("p (t m) -> p m t", t=PACK)
+            nc.vector.tensor_copy(dealt[:, a // PACK : b // PACK, :], table[:].indirect(list_slice(offsets, a, b)))
+
+        def product(tag, t, stationary, moving):
+            bank = psum.tile([P, H], F32, name=f"{tag}{t}", tag=f"{tag}{t}")
+            cols = slice(P * t, P * (t + 1))
+            nc.tensor.matmul_mx(
+                out=bank[:],
+                lhsT=stationary[0][:, cols].bitcast(FP8X4),
+                lhsT_scale=stationary[1][:, cols],
+                rhs=moving[0][:].bitcast(FP8X4),
+                rhs_scale=moving[1][:],
+                start=True,
+                stop=True,
+            )
+            return bank
+
+        xs = sb.tile([P, T], U8, name="xs")
+        nc.vector.memset(xs[:].bitcast(I32), 0)
+        ones = sb.tile([P, 1], F32, name="ones")
+        nc.vector.memset(ones[:], 1.0)
+        preload_sigmoid = sb.tile([P, 1], F32, name="preload_sigmoid")
+        nc.scalar.activation(preload_sigmoid[:], ones[:], ACT.Sigmoid)
+        two_t = load_list("two_t", two)
+        offs_t = load_list("offs_t", offs)
+        wb_raw = load_weight("wb_raw", wb)
+        for q in range(4):
+            nc.sync.dma_start(xs[32 * q : 32 * q + 4, :].bitcast(I32), x_scales[0, 4 * q : 4 * q + 4, :].bitcast(I32))
+        xw = sb.tile([P, T], U32, name="xw")
+        nc.sync.dma_start(xw[:].bitcast(I32), x_words[0].rearrange("p n t -> p (n t)").bitcast(I32))
+        n1_t = load_list("n1_t", n1)
+        wa_raw = load_weight("wa_raw", wa)
+        n2_t = load_list("n2_t", n2)
+        n3_t = load_list("n3_t", n3)
+        n4_t = load_list("n4_t", n4)
+        sl_t = load_rows("sl_t", sl)
+        th_t = load_rows("th_t", th)
+        gi_t = load_rows("gi_t", gi)
+        gt_t = load_rows("gt_t", gt)
+        tau_t = load_rows("tau_t", tau)
+        sl_th = sb.tile([P, PACK], F32, name="sl_th")
+        nc.gpsimd.tensor_tensor(sl_th[:], sl_t[:], th_t[:], ALU.mult)
+        sig_bias = sb.tile([P, PACK], F32, name="sig_bias")
+        nc.gpsimd.tensor_scalar(sig_bias[:], sl_th[:], -1.0, 0.0, ALU.mult, ALU.add)
+        neg_half_gt = sb.tile([P, PACK], F32, name="neg_half_gt")
+        nc.gpsimd.tensor_scalar(neg_half_gt[:], gt_t[:], -0.5, 0.0, ALU.mult, ALU.add)
+        neg_tau = sb.tile([P, PACK], F32, name="neg_tau")
+        nc.gpsimd.tensor_scalar(neg_tau[:], tau_t[:], -1.0, 0.0, ALU.mult, ALU.add)
+
+        x_two = mx_tiles("x_two")
+        x_offs = mx_tiles("x_offs")
+        wb_mx = mx_tiles("wb")
+        wa_mx = mx_tiles("wa")
+        wb_low = interleave("wb_low", nc.scalar.copy, wb_raw[:, :, 0:HALF])
+        wb_high = interleave("wb_high", nc.vector.tensor_copy, wb_raw[:, :, HALF:H])
+        gather_dealt(x_two[1], xs, two_t, 0, S)
+        quantize(wb_mx, HALF, H, wb_high)
+        quantize(wb_mx, 0, HALF, wb_low)
+        gather_dealt(x_two[0], xw, two_t, 0, S)
+        b_bank = [product("low", t, x_two, wb_mx) for t in range(PACK)]
+
+        gather_dealt(x_offs[0], xw, offs_t, 0, S)
+        gather_dealt(x_offs[1], xs, offs_t, 0, S)
+        quantize(wa_mx, 0, H, interleave("staging", nc.vector.tensor_copy, wa_raw[:]))
+        a_bank = [product("high", t, x_offs, wa_mx) for t in range(PACK)]
+
+        b_rows = [sb.tile([P, H], F32, name=f"b{t}") for t in range(PACK)]
+        sg = [sb.tile([P, H], F32, name=f"sg{t}") for t in range(PACK)]
+        for t in range(PACK):
+            if t in ():
+                nc.vector.tensor_copy(b_rows[t][:], b_bank[t][:])
+            else:
+                nc.scalar.copy(b_rows[t][:], b_bank[t][:])
+            for a in range(0, H, HALF):
+                nc.scalar.activation(
+                    sg[t][:, a : a + HALF],
+                    b_rows[t][:].indirect(list_slice(n1_t, a, a + HALF)),
+                    ACT.Sigmoid,
+                    bias=sig_bias[:, t : t + 1],
+                    scale=sl_t[:, t : t + 1],
+                )
+
+        z2_planes = sb.tile([P, PACK, H], BF16, name="z2_planes", tag="staging", align_bytes=64)
+        a_rows = [sb.tile([P, H], F32, name=f"a{t}") for t in range(PACK)]
+        gated = sb.tile([P, PACK, H], F32, name="gated")
+
+        def weigh_b(t):
+            nc.vector.tensor_scalar(z2_planes[:, t, :], b_rows[t][:], gi_t[:, t : t + 1], None, ALU.mult)
+
+        def gate_a(t):
+            nc.vector.scalar_tensor_tensor(gated[:, t, :], a_bank[t][:], gt_t[:, t : t + 1], sg[t][:], ALU.mult, ALU.mult)
+
+        weigh_b(0)
+        weigh_b(1)
+        for t in range(PACK):
+            if t in (3,):
+                nc.scalar.activation(a_rows[t][:], a_bank[t][:], ACT.Copy, scale=neg_half_gt[:, t : t + 1])
+            else:
+                nc.vector.tensor_scalar(a_rows[t][:], a_bank[t][:], neg_half_gt[:, t : t + 1], None, ALU.mult)
+        weigh_b(2)
+        gate_a(0)
+        weigh_b(3)
+        gate_a(1)
+        gate_a(2)
+        gate_a(3)
+        z2_grouped = interleave("z2_grouped", nc.vector.tensor_copy, z2_planes[:])
+        z2_mx = mx_tiles("z2")
+        z_mx = mx_tiles("z")
+        M_HALF = HALF // PACK
+        z_grouped = [sb.tile([P, PACK, M_HALF, PACK], BF16, name=f"z_grouped{h}", align_bytes=64) for h in range(2)]
+
+        def make_z(a, b):
+            fetched = sb.tile([P, PACK, b - a], F32, name=f"fetched{a}")
+            for t in range(PACK):
+                nc.scalar.activation(fetched[:, t, :], a_rows[t][:].indirect(list_slice(n2_t, a, b)), ACT.Copy)
+            h, first = divmod(a, HALF)
+            nc.vector.tensor_tensor(
+                z_grouped[h][:, :, first // PACK : (first + b - a) // PACK, :].rearrange("p s m t -> p m t s"),
+                gated[:, :, a:b].rearrange("p t (m s) -> p m t s", s=PACK),
+                fetched[:].rearrange("p t (m s) -> p m t s", s=PACK),
+                ALU.add,
+            )
+            return fetched
+
+        def quantize_z(h):
+            for s in range(PACK):
+                first = P * s + M_HALF * h
+                quantize(z_mx, first, first + M_HALF, z_grouped[h][:, s, :, :].rearrange("p m t -> p (m t)"))
+
+        make_z(0, 256)
+        quantize(z2_mx, 0, H, z2_grouped)
+        quantize_z(0)
+        make_z(256, 384)
+        last_fetched = make_z(384, 512)
+        quantize_z(1)
+        preload_exp = sb.tile([P, 1], F32, name="preload_exp")
+        nc.scalar.activation(preload_exp[:], last_fetched[:, PACK - 1, 0:1], ACT.Exp, scale=0.0)
+
+        cv_bank = [product("low", s, z_mx, z2_mx) for s in range(PACK)]
+        out_rows = out_0.rearrange("(p s) c -> p s c", s=PACK)
+        result = sb.tile([P, PACK, H], F32, name="result")
+        cv = [sb.tile([P, H], F32, name=f"cv{s}") for s in range(PACK)]
+        ea = [sb.tile([P, H], F32, name=f"ea{s}") for s in range(PACK)]
+        for s in range(PACK):
+            top = sb.tile([P, 1], F32, name=f"top{s}")
+            nc.vector.tensor_scalar(cv[s][:], cv_bank[s][:], 0.0625, None, ALU.mult, ALU.max, accum_out=top[:])
+            exp_bias = sb.tile([P, 1], F32, name=f"exp_bias{s}", tag=f"half_cv{s}")
+            if s == 0:
+                nc.vector.tensor_scalar(exp_bias[:], top[:], neg_tau[:, s : s + 1], None, ALU.mult)
+            else:
+                nc.scalar.activation(exp_bias[:], top[:], ACT.Copy, scale=neg_tau[:, s : s + 1])
+            for a in range(0, H, HALF):
+                nc.scalar.activation(
+                    ea[s][:, a : a + HALF],
+                    cv[s][:].indirect(list_slice(n3_t, a, a + HALF)),
+                    ACT.Exp,
+                    bias=exp_bias[:],
+                    scale=tau_t[:, s : s + 1],
+                )
+        half_cv = [sb.tile([P, H], F32, name=f"half_cv{s}", tag=f"half_cv{s}") for s in range(PACK)]
+        for s in range(PACK):
+            nc.scalar.activation(half_cv[s][:], cv[s][:], ACT.Copy, scale=-0.5)
+
+        ds = [sb.tile([P, 2 * H], F32, name=f"ds{s}") for s in range(PACK)]
+
+        def scatter(s, a, b):
+            nc.vector.tensor_tensor(ds[s][:].indirect(list_slice(n4_t, a, b)), cv[s][:, a:b], ea[s][:, a:b], ALU.mult)
+
+        def combine(s, a, b):
+            nc.vector.scalar_tensor_tensor(result[:, s, a:b], ds[s][:, a:b], 2.0, half_cv[s][:, a:b], ALU.mult, ALU.add)
+
+        def store(s):
+            nc.sync.dma_start(out_rows[:, s, :], result[:, s, :])
+
+        scatter(0, 0, H)
+        scatter(1, 0, H)
+        combine(0, 0, H)
+        store(0)
+        scatter(2, 0, H)
+        combine(1, 0, H)
+        store(1)
+        scatter(3, 0, HALF)
+        combine(2, 0, H)
+        store(2)
+        scatter(3, HALF, H)
+        combine(3, 0, HALF)
+        combine(3, HALF, H)
+        store(3)
+
+        y_mx = mx_tiles("y")
+        y_low = interleave("y_low", nc.scalar.copy, result[:, :, 0:HALF])
+        y_high = interleave("y_high", nc.vector.tensor_copy, result[:, :, HALF:H])
+        words = out_1[0].rearrange("p n t -> p (n t)").bitcast(I32)
+        quantize(y_mx, HALF, H, y_high)
+        nc.sync.dma_start(words[:, HALF:H], y_mx[0][:, HALF:H].bitcast(I32))
+        quantize(y_mx, 0, HALF, y_low)
+        nc.scalar.dma_start(words[:, 0:HALF], y_mx[0][:, 0:HALF].bitcast(I32))
+        for q in range(4):
+            queue = nc.sync if q % 2 == 0 else nc.scalar
+            queue.dma_start(out_2[0, 4 * q : 4 * q + 4, :].bitcast(I32), y_mx[1][32 * q : 32 * q + 4, :].bitcast(I32))

@@ -1,6 +1,7 @@
 from contextlib import ExitStack
 
 import concourse.mybir as mybir
+from concourse.masks import make_identity
 
 K, T, S, H = 512, 2048, 512, 512
 FLOPS = 3 * 2 * 512 * 512 * 512
@@ -39,9 +40,9 @@ def tile_picked_momtgxbesd_none_po_kernel(
             nc.sync.dma_start(tile[:], src)
             return tile
 
-        def load_rows(name, src):
+        def load_rows(name, src, queue):
             tile = sb.tile([P, PACK], F32, name=name)
-            nc.gpsimd.dma_start(tile[:], src.rearrange("(p t) o -> p (t o)", t=PACK))
+            queue.dma_start(tile[:], src.rearrange("(p t) o -> p (t o)", t=PACK))
             return tile
 
         def load_weight(name, src):
@@ -57,9 +58,9 @@ def tile_picked_momtgxbesd_none_po_kernel(
             )
             return grouped[:].rearrange("p c t -> p (c t)")
 
-        def mx_tiles(name):
+        def mx_tiles(name, scale_tag=None):
             codes = sb.tile([P, H], U32, name=f"{name}_codes", align_bytes=64)
-            scales = sb.tile([P, H], U8, name=f"{name}_scales", align_bytes=64)
+            scales = sb.tile([P, H], U8, name=f"{name}_scales", tag=scale_tag or f"{name}_scales", align_bytes=64)
             return codes, scales
 
         def quantize(operand, a, b, grouped):
@@ -94,48 +95,49 @@ def tile_picked_momtgxbesd_none_po_kernel(
         wb_raw = load_weight("wb_raw", wb)
         for q in range(4):
             nc.sync.dma_start(xs[32 * q : 32 * q + 4, :].bitcast(I32), x_scales[0, 4 * q : 4 * q + 4, :].bitcast(I32))
-        xw = sb.tile([P, T], U32, name="xw")
+        xw = sb.tile([P, T], U32, name="xw", align_bytes=64)
         nc.sync.dma_start(xw[:].bitcast(I32), x_words[0].rearrange("p n t -> p (n t)").bitcast(I32))
         n1_t = load_list("n1_t", n1)
         wa_raw = load_weight("wa_raw", wa)
         n2_t = load_list("n2_t", n2)
+        gi_t = load_rows("gi_t", gi, nc.sync)
+        gt_t = load_rows("gt_t", gt, nc.sync)
         n3_t = load_list("n3_t", n3)
         n4_t = load_list("n4_t", n4)
-        sl_t = load_rows("sl_t", sl)
-        th_t = load_rows("th_t", th)
-        gi_t = load_rows("gi_t", gi)
-        gt_t = load_rows("gt_t", gt)
-        tau_t = load_rows("tau_t", tau)
+        tau_t = load_rows("tau_t", tau, nc.sync)
+        sl_t = load_rows("sl_t", sl, nc.gpsimd)
+        th_t = load_rows("th_t", th, nc.gpsimd)
+        identity = sb.tile([P, P], F32, name="identity")
+        make_identity(nc, identity[:])
         sl_th = sb.tile([P, PACK], F32, name="sl_th")
         nc.gpsimd.tensor_tensor(sl_th[:], sl_t[:], th_t[:], ALU.mult)
         sig_bias = sb.tile([P, PACK], F32, name="sig_bias")
         nc.gpsimd.tensor_scalar(sig_bias[:], sl_th[:], -1.0, 0.0, ALU.mult, ALU.add)
-        neg_half_gt = sb.tile([P, PACK], F32, name="neg_half_gt")
-        nc.gpsimd.tensor_scalar(neg_half_gt[:], gt_t[:], -0.5, 0.0, ALU.mult, ALU.add)
         neg_tau = sb.tile([P, PACK], F32, name="neg_tau")
         nc.gpsimd.tensor_scalar(neg_tau[:], tau_t[:], -1.0, 0.0, ALU.mult, ALU.add)
 
         x_two = mx_tiles("x_two")
-        x_offs = mx_tiles("x_offs")
         wb_mx = mx_tiles("wb")
         wa_mx = mx_tiles("wa")
         wb_low = interleave("wb_low", nc.scalar.copy, wb_raw[:, :, 0:HALF])
         wb_high = interleave("wb_high", nc.vector.tensor_copy, wb_raw[:, :, HALF:H])
-        gather_dealt(x_two[1], xs, two_t, 0, S)
         quantize(wb_mx, HALF, H, wb_high)
         quantize(wb_mx, 0, HALF, wb_low)
+        gather_dealt(x_two[1], xs, two_t, 0, S)
         gather_dealt(x_two[0], xw, two_t, 0, S)
         b_bank = [product("low", t, x_two, wb_mx) for t in range(PACK)]
 
+        x_offs = mx_tiles("x_offs", "xw")
         gather_dealt(x_offs[0], xw, offs_t, 0, S)
         gather_dealt(x_offs[1], xs, offs_t, 0, S)
-        quantize(wa_mx, 0, H, interleave("staging", nc.vector.tensor_copy, wa_raw[:]))
+        wa_grouped = interleave("staging", nc.vector.tensor_copy, wa_raw[:])
+        quantize(wa_mx, 0, H, wa_grouped)
         a_bank = [product("high", t, x_offs, wa_mx) for t in range(PACK)]
 
-        b_rows = [sb.tile([P, H], F32, name=f"b{t}") for t in range(PACK)]
-        sg = [sb.tile([P, H], F32, name=f"sg{t}") for t in range(PACK)]
+        b_rows = [sb.tile([P, H], F32, name=f"b{t}", tag="wa_raw" if t == PACK - 1 else f"b{t}") for t in range(PACK)]
+        sg = [sb.tile([P, H], F32, name=f"sg{t}", align_bytes=64) for t in range(PACK)]
         for t in range(PACK):
-            if t in ():
+            if t in (3,):
                 nc.vector.tensor_copy(b_rows[t][:], b_bank[t][:])
             else:
                 nc.scalar.copy(b_rows[t][:], b_bank[t][:])
@@ -153,7 +155,8 @@ def tile_picked_momtgxbesd_none_po_kernel(
         gated = sb.tile([P, PACK, H], F32, name="gated")
 
         def weigh_b(t):
-            nc.vector.tensor_scalar(z2_planes[:, t, :], b_rows[t][:], gi_t[:, t : t + 1], None, ALU.mult)
+            engine = nc.vector if t < 2 else nc.gpsimd
+            engine.tensor_scalar(z2_planes[:, t, :], b_rows[t][:], gi_t[:, t : t + 1], 0.0, ALU.mult, ALU.add)
 
         def gate_a(t):
             nc.vector.scalar_tensor_tensor(gated[:, t, :], a_bank[t][:], gt_t[:, t : t + 1], sg[t][:], ALU.mult, ALU.mult)
@@ -161,31 +164,35 @@ def tile_picked_momtgxbesd_none_po_kernel(
         weigh_b(0)
         weigh_b(1)
         for t in range(PACK):
-            if t in (3,):
-                nc.scalar.activation(a_rows[t][:], a_bank[t][:], ACT.Copy, scale=neg_half_gt[:, t : t + 1])
+            if t in ():
+                nc.scalar.activation(a_rows[t][:], a_bank[t][:], ACT.Copy, scale=gt_t[:, t : t + 1])
             else:
-                nc.vector.tensor_scalar(a_rows[t][:], a_bank[t][:], neg_half_gt[:, t : t + 1], None, ALU.mult)
+                nc.vector.tensor_scalar(a_rows[t][:], a_bank[t][:], gt_t[:, t : t + 1], None, ALU.mult)
         weigh_b(2)
         gate_a(0)
         weigh_b(3)
         gate_a(1)
         gate_a(2)
         gate_a(3)
-        z2_grouped = interleave("z2_grouped", nc.vector.tensor_copy, z2_planes[:])
+        def gpsimd_copy(out, in_):
+            nc.gpsimd.tensor_scalar(out, in_, 1.0, 0.0, ALU.mult, ALU.add)
+
+        z2_grouped = sb.tile([P, H, PACK], BF16, name="z2_grouped", align_bytes=64)
+        gpsimd_copy(z2_grouped[:], z2_planes[:].rearrange("p t c -> p c t"))
+        z2_grouped = z2_grouped[:].rearrange("p c t -> p (c t)")
         z2_mx = mx_tiles("z2")
         z_mx = mx_tiles("z")
         M_HALF = HALF // PACK
-        z_grouped = [sb.tile([P, PACK, M_HALF, PACK], BF16, name=f"z_grouped{h}", align_bytes=64) for h in range(2)]
+        z_grouped = [sb.tile([P, PACK, M_HALF, PACK], BF16, name=f"z_grouped{h}", tag=("z2_grouped", "z_grouped1")[h], align_bytes=64) for h in range(2)]
 
-        def make_z(a, b):
-            fetched = sb.tile([P, PACK, b - a], F32, name=f"fetched{a}")
+        def make_z(a, b, fetched):
             for t in range(PACK):
-                nc.scalar.activation(fetched[:, t, :], a_rows[t][:].indirect(list_slice(n2_t, a, b)), ACT.Copy)
+                nc.scalar.activation(fetched[:, t, :], a_rows[t][:].indirect(list_slice(n2_t, a, b)), ACT.Copy, scale=-0.5)
             h, first = divmod(a, HALF)
             nc.vector.tensor_tensor(
                 z_grouped[h][:, :, first // PACK : (first + b - a) // PACK, :].rearrange("p s m t -> p m t s"),
                 gated[:, :, a:b].rearrange("p t (m s) -> p m t s", s=PACK),
-                fetched[:].rearrange("p t (m s) -> p m t s", s=PACK),
+                fetched.rearrange("p t (m s) -> p m t s", s=PACK),
                 ALU.add,
             )
             return fetched
@@ -195,11 +202,13 @@ def tile_picked_momtgxbesd_none_po_kernel(
                 first = P * s + M_HALF * h
                 quantize(z_mx, first, first + M_HALF, z_grouped[h][:, s, :, :].rearrange("p m t -> p (m t)"))
 
-        make_z(0, 256)
         quantize(z2_mx, 0, H, z2_grouped)
+        fetched_early = sb.tile([P, PACK, HALF], F32, name="fetched_early")
+        make_z(0, 256, fetched_early[:])
         quantize_z(0)
-        make_z(256, 384)
-        last_fetched = make_z(384, 512)
+        fetched_late = sb.tile([P, 2, PACK, P], F32, name="fetched_late", tag="sg3", align_bytes=64)
+        make_z(256, 384, fetched_late[:, 0, :, :])
+        last_fetched = make_z(384, 512, fetched_late[:, 1, :, :])
         quantize_z(1)
         preload_exp = sb.tile([P, 1], F32, name="preload_exp")
         nc.scalar.activation(preload_exp[:], last_fetched[:, PACK - 1, 0:1], ACT.Exp, scale=0.0)
@@ -225,35 +234,43 @@ def tile_picked_momtgxbesd_none_po_kernel(
                     bias=exp_bias[:],
                     scale=tau_t[:, s : s + 1],
                 )
-        half_cv = [sb.tile([P, H], F32, name=f"half_cv{s}", tag=f"half_cv{s}") for s in range(PACK)]
+        ON_TENSOR = 3
+        part_cv = [sb.tile([P, H], F32, name=f"part_cv{s}", tag=f"half_cv{s}") for s in range(PACK)]
         for s in range(PACK):
-            nc.scalar.activation(half_cv[s][:], cv[s][:], ACT.Copy, scale=-0.5)
+            nc.scalar.activation(part_cv[s][:], cv[s][:], ACT.Copy, scale=-0.25 if s < ON_TENSOR else -0.5)
 
         ds = [sb.tile([P, 2 * H], F32, name=f"ds{s}") for s in range(PACK)]
 
-        def scatter(s, a, b):
-            nc.vector.tensor_tensor(ds[s][:].indirect(list_slice(n4_t, a, b)), cv[s][:, a:b], ea[s][:, a:b], ALU.mult)
+        def combine_on_tensor(s):
+            turned = []
+            for h in range(2):
+                sums = psum.tile([P, 2, P], F32, name=f"sums{s}{h}", tag=f"high{h}")
+                for c in range(2):
+                    cols = slice(HALF * h + P * c, HALF * h + P * (c + 1))
+                    nc.tensor.matmul(sums[:, c, :], ds[s][:, cols], identity[:], start=True, stop=False, is_transpose=True)
+                    nc.tensor.matmul(sums[:, c, :], part_cv[s][:, cols], identity[:], start=False, stop=True, is_transpose=True)
+                doubled = sb.tile([P, 2, P], F32, name=f"doubled{s}{h}")
+                nc.scalar.activation(doubled[:], sums[:], ACT.Copy, scale=2.0)
+                turned.append(doubled)
+            for h in range(2):
+                back = psum.tile([P, 2, P], F32, name=f"back{s}{h}", tag=f"high{2 + h}")
+                for c in range(2):
+                    nc.tensor.transpose(back[:, c, :], turned[h][:, c, :], identity[:])
+                nc.scalar.copy(result[:, s, HALF * h : HALF * (h + 1)], back[:].rearrange("p c n -> p (c n)"))
 
         def combine(s, a, b):
-            nc.vector.scalar_tensor_tensor(result[:, s, a:b], ds[s][:, a:b], 2.0, half_cv[s][:, a:b], ALU.mult, ALU.add)
+            nc.vector.scalar_tensor_tensor(result[:, s, a:b], ds[s][:, a:b], 2.0, part_cv[s][:, a:b], ALU.mult, ALU.add)
 
-        def store(s):
-            nc.sync.dma_start(out_rows[:, s, :], result[:, s, :])
-
-        scatter(0, 0, H)
-        scatter(1, 0, H)
-        combine(0, 0, H)
-        store(0)
-        scatter(2, 0, H)
-        combine(1, 0, H)
-        store(1)
-        scatter(3, 0, HALF)
-        combine(2, 0, H)
-        store(2)
-        scatter(3, HALF, H)
-        combine(3, 0, HALF)
-        combine(3, HALF, H)
-        store(3)
+        for s in range(PACK):
+            nc.vector.tensor_tensor(ds[s][:].indirect(n4_t[:]), cv[s][:], ea[s][:], ALU.mult)
+            if s < ON_TENSOR:
+                combine_on_tensor(s)
+            else:
+                combine(s, 0, HALF)
+                combine(s, HALF, H)
+            if s < 2:
+                nc.sync.dma_start(out_rows[:, s, :], result[:, s, :])
+        nc.sync.dma_start(out_rows[:, 2:4, :], result[:, 2:4, :])
 
         y_mx = mx_tiles("y")
         y_low = interleave("y_low", nc.scalar.copy, result[:, :, 0:HALF])

@@ -134,10 +134,10 @@ def tile_picked_momtgxbesd_none_po_kernel(
         quantize(wa_mx, 0, H, wa_grouped)
         a_bank = [product("high", t, x_offs, wa_mx) for t in range(PACK)]
 
-        b_rows = [sb.tile([P, H], F32, name=f"b{t}", tag="wa_raw" if t == PACK - 1 else f"b{t}") for t in range(PACK)]
+        b_rows = [sb.tile([P, H], F32, name=f"b{t}") for t in range(PACK)]
         sg = [sb.tile([P, H], F32, name=f"sg{t}", align_bytes=64) for t in range(PACK)]
         for t in range(PACK):
-            if t in (3,):
+            if t in ():
                 nc.vector.tensor_copy(b_rows[t][:], b_bank[t][:])
             else:
                 nc.scalar.copy(b_rows[t][:], b_bank[t][:])
@@ -155,8 +155,7 @@ def tile_picked_momtgxbesd_none_po_kernel(
         gated = sb.tile([P, PACK, H], F32, name="gated")
 
         def weigh_b(t):
-            engine = nc.vector if t < 2 else nc.gpsimd
-            engine.tensor_scalar(z2_planes[:, t, :], b_rows[t][:], gi_t[:, t : t + 1], 0.0, ALU.mult, ALU.add)
+            nc.vector.tensor_scalar(z2_planes[:, t, :], b_rows[t][:], gi_t[:, t : t + 1], None, ALU.mult)
 
         def gate_a(t):
             nc.vector.scalar_tensor_tensor(gated[:, t, :], a_bank[t][:], gt_t[:, t : t + 1], sg[t][:], ALU.mult, ALU.mult)
@@ -164,7 +163,7 @@ def tile_picked_momtgxbesd_none_po_kernel(
         weigh_b(0)
         weigh_b(1)
         for t in range(PACK):
-            if t in ():
+            if t in (3,):
                 nc.scalar.activation(a_rows[t][:], a_bank[t][:], ACT.Copy, scale=gt_t[:, t : t + 1])
             else:
                 nc.vector.tensor_scalar(a_rows[t][:], a_bank[t][:], gt_t[:, t : t + 1], None, ALU.mult)
@@ -174,42 +173,30 @@ def tile_picked_momtgxbesd_none_po_kernel(
         gate_a(1)
         gate_a(2)
         gate_a(3)
-        def gpsimd_copy(out, in_):
-            nc.gpsimd.tensor_scalar(out, in_, 1.0, 0.0, ALU.mult, ALU.add)
-
-        z2_grouped = sb.tile([P, H, PACK], BF16, name="z2_grouped", align_bytes=64)
-        gpsimd_copy(z2_grouped[:], z2_planes[:].rearrange("p t c -> p c t"))
-        z2_grouped = z2_grouped[:].rearrange("p c t -> p (c t)")
+        z2_grouped = interleave("z2_grouped", nc.vector.tensor_copy, z2_planes[:])
         z2_mx = mx_tiles("z2")
         z_mx = mx_tiles("z")
-        M_HALF = HALF // PACK
-        z_grouped = [sb.tile([P, PACK, M_HALF, PACK], BF16, name=f"z_grouped{h}", tag=("z2_grouped", "z_grouped1")[h], align_bytes=64) for h in range(2)]
+        z_grouped = sb.tile([P, PACK, P, PACK], BF16, name="z_grouped", align_bytes=64)
 
         def make_z(a, b, fetched):
             for t in range(PACK):
                 nc.scalar.activation(fetched[:, t, :], a_rows[t][:].indirect(list_slice(n2_t, a, b)), ACT.Copy, scale=-0.5)
-            h, first = divmod(a, HALF)
             nc.vector.tensor_tensor(
-                z_grouped[h][:, :, first // PACK : (first + b - a) // PACK, :].rearrange("p s m t -> p m t s"),
+                z_grouped[:, :, a // PACK : b // PACK, :].rearrange("p s m t -> p m t s"),
                 gated[:, :, a:b].rearrange("p t (m s) -> p m t s", s=PACK),
                 fetched.rearrange("p t (m s) -> p m t s", s=PACK),
                 ALU.add,
             )
             return fetched
 
-        def quantize_z(h):
-            for s in range(PACK):
-                first = P * s + M_HALF * h
-                quantize(z_mx, first, first + M_HALF, z_grouped[h][:, s, :, :].rearrange("p m t -> p (m t)"))
-
         quantize(z2_mx, 0, H, z2_grouped)
         fetched_early = sb.tile([P, PACK, HALF], F32, name="fetched_early")
         make_z(0, 256, fetched_early[:])
-        quantize_z(0)
         fetched_late = sb.tile([P, 2, PACK, P], F32, name="fetched_late", tag="sg3", align_bytes=64)
         make_z(256, 384, fetched_late[:, 0, :, :])
         last_fetched = make_z(384, 512, fetched_late[:, 1, :, :])
-        quantize_z(1)
+        for s in range(PACK):
+            quantize(z_mx, P * s, P * (s + 1), z_grouped[:, s, :, :].rearrange("p m t -> p (m t)"))
         preload_exp = sb.tile([P, 1], F32, name="preload_exp")
         nc.scalar.activation(preload_exp[:], last_fetched[:, PACK - 1, 0:1], ACT.Exp, scale=0.0)
 
@@ -222,10 +209,7 @@ def tile_picked_momtgxbesd_none_po_kernel(
             top = sb.tile([P, 1], F32, name=f"top{s}")
             nc.vector.tensor_scalar(cv[s][:], cv_bank[s][:], 0.0625, None, ALU.mult, ALU.max, accum_out=top[:])
             exp_bias = sb.tile([P, 1], F32, name=f"exp_bias{s}", tag=f"half_cv{s}")
-            if s == 0:
-                nc.vector.tensor_scalar(exp_bias[:], top[:], neg_tau[:, s : s + 1], None, ALU.mult)
-            else:
-                nc.scalar.activation(exp_bias[:], top[:], ACT.Copy, scale=neg_tau[:, s : s + 1])
+            nc.scalar.activation(exp_bias[:], top[:], ACT.Copy, scale=neg_tau[:, s : s + 1])
             for a in range(0, H, HALF):
                 nc.scalar.activation(
                     ea[s][:, a : a + HALF],

from contextlib import ExitStack

import concourse.mybir as mybir
from concourse.masks import make_identity

K, T, S, H = 512, 2048, 512, 512
FLOPS = 3 * 2 * 512 * 512 * 512

F32 = mybir.dt.float32
BF16 = mybir.dt.bfloat16
I32 = mybir.dt.int32
U32 = mybir.dt.uint32
U16 = mybir.dt.uint16
U8 = mybir.dt.uint8
FP8X4 = mybir.dt.float8_e4m3fn_x4
ALU = mybir.AluOpType
ACT = mybir.ActivationFunctionType

P = 128
PACK = 4
HALF = H // 2
LIST_COLS = S // 16


def list_slice(offsets, a, b):
    return offsets[:, a // 16 : b // 16]


def tile_picked_momtgxbesd_none_po_kernel(
    tc, x_words, x_scales, wa, wb, sl, th, gt, gi, tau, offs, two, n1, n2, n3, n4, out_0, out_1, out_2
):
    nc = tc.nc
    with ExitStack() as ctx:
        lists = ctx.enter_context(tc.tile_pool(name="lists", bufs=1))
        sb = ctx.enter_context(tc.tile_pool(name="sb", bufs=1))
        psum = ctx.enter_context(tc.psum_pool(name="psum", bufs=1))

        def load_list(name, src):
            tile = lists.tile([P, LIST_COLS], U16, name=name)
            nc.sync.dma_start(tile[:], src)
            return tile

        def load_rows(name, src, queue):
            tile = sb.tile([P, PACK], F32, name=name)
            queue.dma_start(tile[:], src.rearrange("(p t) o -> p (t o)", t=PACK))
            return tile

        def load_weight(name, src):
            tile = sb.tile([P, PACK, H], F32, name=name)
            nc.sync.dma_start(tile[:], src.rearrange("(p j) c -> p j c", j=PACK))
            return tile

        def interleave(name, copy, planes):
            grouped = sb.tile([P, planes.shape[2], PACK], BF16, name=name, align_bytes=64)
            copy(
                grouped[:].rearrange("p (c i) t -> p c t i", i=4),
                planes.rearrange("p t (c i) -> p c t i", i=4),
            )
            return grouped[:].rearrange("p c t -> p (c t)")

        def mx_tiles(name, scale_tag=None):
            codes = sb.tile([P, H], U32, name=f"{name}_codes", align_bytes=64)
            scales = sb.tile([P, H], U8, name=f"{name}_scales", tag=scale_tag or f"{name}_scales", align_bytes=64)
            return codes, scales

        def quantize(operand, a, b, grouped):
            nc.vector.quantize_mx(out=operand[0][:, a:b].bitcast(FP8X4), scales=operand[1][:, a:b], in_=grouped)

        def gather_dealt(picked, table, offsets, a, b):
            dealt = picked[:].rearrange("p (t m) -> p m t", t=PACK)
            nc.vector.tensor_copy(dealt[:, a // PACK : b // PACK, :], table[:].indirect(list_slice(offsets, a, b)))

        def product(tag, t, stationary, moving):
            bank = psum.tile([P, H], F32, name=f"{tag}{t}", tag=f"{tag}{t}")
            cols = slice(P * t, P * (t + 1))
            nc.tensor.matmul_mx(
                out=bank[:],
                lhsT=stationary[0][:, cols].bitcast(FP8X4),
                lhsT_scale=stationary[1][:, cols],
                rhs=moving[0][:].bitcast(FP8X4),
                rhs_scale=moving[1][:],
                start=True,
                stop=True,
            )
            return bank

        xs = sb.tile([P, T], U8, name="xs")
        nc.vector.memset(xs[:].bitcast(I32), 0)
        ones = sb.tile([P, 1], F32, name="ones")
        nc.vector.memset(ones[:], 1.0)
        preload_sigmoid = sb.tile([P, 1], F32, name="preload_sigmoid")
        nc.scalar.activation(preload_sigmoid[:], ones[:], ACT.Sigmoid)
        two_t = load_list("two_t", two)
        offs_t = load_list("offs_t", offs)
        wb_raw = load_weight("wb_raw", wb)
        for q in range(4):
            nc.sync.dma_start(xs[32 * q : 32 * q + 4, :].bitcast(I32), x_scales[0, 4 * q : 4 * q + 4, :].bitcast(I32))
        xw = sb.tile([P, T], U32, name="xw", align_bytes=64)
        nc.sync.dma_start(xw[:].bitcast(I32), x_words[0].rearrange("p n t -> p (n t)").bitcast(I32))
        n1_t = load_list("n1_t", n1)
        wa_raw = load_weight("wa_raw", wa)
        n2_t = load_list("n2_t", n2)
        gi_t = load_rows("gi_t", gi, nc.sync)
        gt_t = load_rows("gt_t", gt, nc.sync)
        n3_t = load_list("n3_t", n3)
        n4_t = load_list("n4_t", n4)
        tau_t = load_rows("tau_t", tau, nc.sync)
        sl_t = load_rows("sl_t", sl, nc.gpsimd)
        th_t = load_rows("th_t", th, nc.gpsimd)
        identity = sb.tile([P, P], F32, name="identity")
        make_identity(nc, identity[:])
        sl_th = sb.tile([P, PACK], F32, name="sl_th")
        nc.gpsimd.tensor_tensor(sl_th[:], sl_t[:], th_t[:], ALU.mult)
        sig_bias = sb.tile([P, PACK], F32, name="sig_bias")
        nc.gpsimd.tensor_scalar(sig_bias[:], sl_th[:], -1.0, 0.0, ALU.mult, ALU.add)
        neg_tau = sb.tile([P, PACK], F32, name="neg_tau")
        nc.gpsimd.tensor_scalar(neg_tau[:], tau_t[:], -1.0, 0.0, ALU.mult, ALU.add)

        x_two = mx_tiles("x_two")
        wb_mx = mx_tiles("wb")
        wa_mx = mx_tiles("wa")
        wb_low = interleave("wb_low", nc.scalar.copy, wb_raw[:, :, 0:HALF])
        wb_high = interleave("wb_high", nc.vector.tensor_copy, wb_raw[:, :, HALF:H])
        quantize(wb_mx, HALF, H, wb_high)
        quantize(wb_mx, 0, HALF, wb_low)
        gather_dealt(x_two[1], xs, two_t, 0, S)
        gather_dealt(x_two[0], xw, two_t, 0, S)
        b_bank = [product("low", t, x_two, wb_mx) for t in range(PACK)]

        x_offs = mx_tiles("x_offs", "xw")
        gather_dealt(x_offs[0], xw, offs_t, 0, S)
        gather_dealt(x_offs[1], xs, offs_t, 0, S)
        wa_grouped = interleave("staging", nc.vector.tensor_copy, wa_raw[:])
        quantize(wa_mx, 0, H, wa_grouped)
        a_bank = [product("high", t, x_offs, wa_mx) for t in range(PACK)]

        b_rows = [sb.tile([P, H], F32, name=f"b{t}") for t in range(PACK)]
        sg = [sb.tile([P, H], F32, name=f"sg{t}", align_bytes=64) for t in range(PACK)]
        for t in range(PACK):
            if t in ():
                nc.vector.tensor_copy(b_rows[t][:], b_bank[t][:])
            else:
                nc.scalar.copy(b_rows[t][:], b_bank[t][:])
            for a in range(0, H, HALF):
                nc.scalar.activation(
                    sg[t][:, a : a + HALF],
                    b_rows[t][:].indirect(list_slice(n1_t, a, a + HALF)),
                    ACT.Sigmoid,
                    bias=sig_bias[:, t : t + 1],
                    scale=sl_t[:, t : t + 1],
                )

        z2_planes = sb.tile([P, PACK, H], BF16, name="z2_planes", tag="staging", align_bytes=64)
        a_rows = [sb.tile([P, H], F32, name=f"a{t}") for t in range(PACK)]
        gated = sb.tile([P, PACK, H], F32, name="gated")

        def weigh_b(t):
            nc.vector.tensor_scalar(z2_planes[:, t, :], b_rows[t][:], gi_t[:, t : t + 1], None, ALU.mult)

        def gate_a(t):
            nc.vector.scalar_tensor_tensor(gated[:, t, :], a_bank[t][:], gt_t[:, t : t + 1], sg[t][:], ALU.mult, ALU.mult)

        weigh_b(0)
        weigh_b(1)
        for t in range(PACK):
            if t in (3,):
                nc.scalar.activation(a_rows[t][:], a_bank[t][:], ACT.Copy, scale=gt_t[:, t : t + 1])
            else:
                nc.vector.tensor_scalar(a_rows[t][:], a_bank[t][:], gt_t[:, t : t + 1], None, ALU.mult)
        weigh_b(2)
        gate_a(0)
        weigh_b(3)
        gate_a(1)
        gate_a(2)
        gate_a(3)
        z2_grouped = interleave("z2_grouped", nc.vector.tensor_copy, z2_planes[:])
        z2_mx = mx_tiles("z2")
        z_mx = mx_tiles("z")
        z_grouped = sb.tile([P, PACK, P, PACK], BF16, name="z_grouped", align_bytes=64)

        def make_z(a, b, fetched):
            for t in range(PACK):
                nc.scalar.activation(fetched[:, t, :], a_rows[t][:].indirect(list_slice(n2_t, a, b)), ACT.Copy, scale=-0.5)
            nc.vector.tensor_tensor(
                z_grouped[:, :, a // PACK : b // PACK, :].rearrange("p s m t -> p m t s"),
                gated[:, :, a:b].rearrange("p t (m s) -> p m t s", s=PACK),
                fetched.rearrange("p t (m s) -> p m t s", s=PACK),
                ALU.add,
            )
            return fetched

        quantize(z2_mx, 0, H, z2_grouped)
        fetched_early = sb.tile([P, PACK, HALF], F32, name="fetched_early")
        make_z(0, 256, fetched_early[:])
        fetched_late = sb.tile([P, 2, PACK, P], F32, name="fetched_late", tag="sg3", align_bytes=64)
        make_z(256, 384, fetched_late[:, 0, :, :])
        last_fetched = make_z(384, 512, fetched_late[:, 1, :, :])
        for s in range(PACK):
            quantize(z_mx, P * s, P * (s + 1), z_grouped[:, s, :, :].rearrange("p m t -> p (m t)"))
        preload_exp = sb.tile([P, 1], F32, name="preload_exp")
        nc.scalar.activation(preload_exp[:], last_fetched[:, PACK - 1, 0:1], ACT.Exp, scale=0.0)

        cv_bank = [product("low", s, z_mx, z2_mx) for s in range(PACK)]
        out_rows = out_0.rearrange("(p s) c -> p s c", s=PACK)
        result = sb.tile([P, PACK, H], F32, name="result")
        cv = [sb.tile([P, H], F32, name=f"cv{s}") for s in range(PACK)]
        ea = [sb.tile([P, H], F32, name=f"ea{s}") for s in range(PACK)]
        for s in range(PACK):
            top = sb.tile([P, 1], F32, name=f"top{s}")
            nc.vector.tensor_scalar(cv[s][:], cv_bank[s][:], 0.0625, None, ALU.mult, ALU.max, accum_out=top[:])
            exp_bias = sb.tile([P, 1], F32, name=f"exp_bias{s}", tag=f"half_cv{s}")
            nc.scalar.activation(exp_bias[:], top[:], ACT.Copy, scale=neg_tau[:, s : s + 1])
            for a in range(0, H, HALF):
                nc.scalar.activation(
                    ea[s][:, a : a + HALF],
                    cv[s][:].indirect(list_slice(n3_t, a, a + HALF)),
                    ACT.Exp,
                    bias=exp_bias[:],
                    scale=tau_t[:, s : s + 1],
                )
        ON_TENSOR = 3
        part_cv = [sb.tile([P, H], F32, name=f"part_cv{s}", tag=f"half_cv{s}") for s in range(PACK)]
        for s in range(PACK):
            nc.scalar.activation(part_cv[s][:], cv[s][:], ACT.Copy, scale=-0.25 if s < ON_TENSOR else -0.5)

        ds = [sb.tile([P, 2 * H], F32, name=f"ds{s}") for s in range(PACK)]

        def combine_on_tensor(s):
            turned = []
            for h in range(2):
                sums = psum.tile([P, 2, P], F32, name=f"sums{s}{h}", tag=f"high{h}")
                for c in range(2):
                    cols = slice(HALF * h + P * c, HALF * h + P * (c + 1))
                    nc.tensor.matmul(sums[:, c, :], ds[s][:, cols], identity[:], start=True, stop=False, is_transpose=True)
                    nc.tensor.matmul(sums[:, c, :], part_cv[s][:, cols], identity[:], start=False, stop=True, is_transpose=True)
                doubled = sb.tile([P, 2, P], F32, name=f"doubled{s}{h}")
                nc.scalar.activation(doubled[:], sums[:], ACT.Copy, scale=2.0)
                turned.append(doubled)
            for h in range(2):
                back = psum.tile([P, 2, P], F32, name=f"back{s}{h}", tag=f"high{2 + h}")
                for c in range(2):
                    nc.tensor.transpose(back[:, c, :], turned[h][:, c, :], identity[:])
                nc.scalar.copy(result[:, s, HALF * h : HALF * (h + 1)], back[:].rearrange("p c n -> p (c n)"))

        def combine(s, a, b):
            nc.vector.scalar_tensor_tensor(result[:, s, a:b], ds[s][:, a:b], 2.0, part_cv[s][:, a:b], ALU.mult, ALU.add)

        for s in range(PACK):
            nc.vector.tensor_tensor(ds[s][:].indirect(n4_t[:]), cv[s][:], ea[s][:], ALU.mult)
            if s < ON_TENSOR:
                combine_on_tensor(s)
            else:
                combine(s, 0, HALF)
                combine(s, HALF, H)
            if s < 2:
                nc.sync.dma_start(out_rows[:, s, :], result[:, s, :])
        nc.sync.dma_start(out_rows[:, 2:4, :], result[:, 2:4, :])

        y_mx = mx_tiles("y")
        y_low = interleave("y_low", nc.scalar.copy, result[:, :, 0:HALF])
        y_high = interleave("y_high", nc.vector.tensor_copy, result[:, :, HALF:H])
        words = out_1[0].rearrange("p n t -> p (n t)").bitcast(I32)
        quantize(y_mx, HALF, H, y_high)
        nc.sync.dma_start(words[:, HALF:H], y_mx[0][:, HALF:H].bitcast(I32))
        quantize(y_mx, 0, HALF, y_low)
        nc.scalar.dma_start(words[:, 0:HALF], y_mx[0][:, 0:HALF].bitcast(I32))
        for q in range(4):
            queue = nc.sync if q % 2 == 0 else nc.scalar
            queue.dma_start(out_2[0, 4 * q : 4 * q + 4, :].bitcast(I32), y_mx[1][32 * q : 32 * q + 4, :].bitcast(I32))
